import numpy as np
import ml_dtypes


def mxq(x, axis, fmt="e4m3"):
    dtype, down = {"e4m3": (ml_dtypes.float8_e4m3fn, 7), "e5m2": (ml_dtypes.float8_e5m2, 14)}[fmt]
    v = np.moveaxis(np.asarray(x, np.float32).astype(ml_dtypes.bfloat16).astype(np.float64), axis, -1)
    blocks = v.reshape(v.shape[:-1] + (-1, 32))
    amax = np.abs(blocks).max(-1, keepdims=True)
    byte = np.maximum(np.where(amax > 0, np.frexp(amax)[1] - 1 + 127, 0) - down, 1)
    scale = np.exp2(byte - 127.0)
    codes = (blocks / scale).astype(np.float32).astype(dtype).astype(np.float64)
    return np.moveaxis((codes * scale).reshape(v.shape), -1, axis)


WIDE = False


def mx_kscale(k):
    if not WIDE:
        return np.ones(k)
    levels = np.array([30, -30])
    if k % 512:
        return np.exp2(np.random.permutation(np.resize(levels, k // 32))).repeat(32)
    a = np.empty((k // 512, 16))
    for p in range(k // 512):
        a[p, :8] = np.random.permutation(np.resize(levels, 8))
        for g in range(8):
            far = levels[np.abs(levels - a[p, g]) >= 10]
            a[p, g + 8] = far[np.random.randint(len(far))]
    return np.exp2(a.ravel()).repeat(32)


def f64(x):
    return np.asarray(x).astype(np.float64)


T, D, H = 1024, 256, 1536


def setup_inputs():
    n = np.random.standard_normal
    s1 = mx_kscale(T)[:, None]
    s2 = mx_kscale(T)[:, None]
    m = np.exp(0.5 * n((T, 1)))
    return {
        "x": (n((T, D)) * s1).astype(np.float32),
        "de": (m * n((T, H)) / np.sqrt(T) / s1).astype(np.float32),
        "dr": (m * n((T, D)) / np.sqrt(T) * s2).astype(np.float32),
        "e": (n((T, H)) / s2).astype(np.float32),
        "g0": (n((256, 1536))).astype(np.float32),
    }


def reference(x, de, dr, e, g0):
    x_ = mxq(f64(x), 0, "e4m3")
    de_ = mxq(f64(de), 0, "e5m2")
    dr_ = mxq(f64(dr), 0, "e5m2")
    e_ = mxq(f64(e), 0, "e4m3")
    y = x_.T @ de_ + dr_.T @ e_
    return f64(g0) + y

from contextlib import ExitStack

import concourse.mybir as mybir

T, D, H = 1024, 256, 1536
FLOPS = 2 * 2 * T * D * H

F32 = mybir.dt.float32
BF16 = mybir.dt.bfloat16
U32 = mybir.dt.uint32
U8 = mybir.dt.uint8
E4M3 = mybir.dt.float8_e4m3fn_x4
E5M2 = mybir.dt.float8_e5m2_x4

P = 128
PACK = 4
K_PASS = P * PACK
PASSES = T // K_PASS
N_TILE = 512
H_TILES = H // N_TILE
D_TILES = D // P


def tile_mix_tied_res_kernel(tc, x, de, dr, e, g0, out):
    nc = tc.nc

    def interleave(copy, grouped, raw, c0, c1, j0=0):
        rows = raw.shape[1]
        copy(
            out=grouped[:, c0:c1, j0 : j0 + rows].rearrange("p (c i) j -> p c j i", i=4),
            in_=raw[:, :, c0:c1].rearrange("p j (c i) -> p c j i", i=4),
        )

    with ExitStack() as ctx:
        keep = ctx.enter_context(tc.tile_pool(name="keep", bufs=1))
        psum = ctx.enter_context(tc.psum_pool(name="psum", bufs=1))
        ctx.enter_context(tc.manual_schedule())

        def narrow_tiles(name):
            raw = keep.tile([P, PASSES, PACK, D], F32, name=name + "_raw", align_bytes=64)
            grouped = keep.tile([P, PASSES, D, PACK], BF16, name=name + "_grouped", align_bytes=64)
            codes = keep.tile([P, PASSES * D], U32, name=name + "_codes", align_bytes=64)
            scales = keep.tile([P, PASSES * D], U8, name=name + "_scales", align_bytes=64)
            return raw, grouped, codes, scales

        def wide_tiles(name):
            grouped = keep.tile([P, H, PACK], BF16, name=name + "_grouped", align_bytes=64)
            codes = keep.tile([P, H], U32, name=name + "_codes", align_bytes=64)
            scales = keep.tile([P, H], U8, name=name + "_scales", align_bytes=64)
            return grouped, codes, scales

        def load_narrow(t, src):
            nc.sync.dma_start(out=t[0][:], in_=src.rearrange("(c p j) d -> p c j d", p=P, j=PACK))

        def load_wide(src, c, j0, j1, name):
            raw = keep.tile([P, j1 - j0, H], F32, name=name, align_bytes=64)
            rows = src[c * K_PASS : (c + 1) * K_PASS, :].rearrange("(p j) h -> p j h", j=PACK)
            nc.sync.dma_start(out=raw[:], in_=rows[:, j0:j1, :])
            return raw

        xt = narrow_tiles("x")
        drt = narrow_tiles("dr")
        load_narrow(xt, x)
        de0 = load_wide(de, 0, 0, 4, "de0")
        de1 = load_wide(de, 1, 0, 4, "de1")
        load_narrow(drt, dr)
        e0 = load_wide(e, 0, 0, 4, "e0")
        e1a = load_wide(e, 1, 0, 2, "e1a")
        e1b = load_wide(e, 1, 2, 4, "e1b")
        g = []
        for d in range(D_TILES):
            gt = keep.tile([P, H], F32, name="g%d" % d)
            nc.sync.dma_start(out=gt[:], in_=g0[d * P : (d + 1) * P, :])
            g.append(gt)

        acc = [
            [psum.tile([P, N_TILE], F32, name="acc%d%d" % (d, h)) for h in range(H_TILES)]
            for d in range(D_TILES)
        ]

        def quant_narrow(t, fmt):
            raw, grouped, codes, scales = t
            interleave(nc.vector.tensor_copy, grouped[:, 0, :, :], raw[:, 0, :, :], 0, D)
            interleave(nc.scalar.copy, grouped[:, 1, :, :], raw[:, 1, :, :], 0, D)
            nc.vector.quantize_mx(
                out=codes[:].bitcast(fmt),
                scales=scales[:],
                in_=grouped[:].rearrange("p c d j -> p (c d j)"),
            )

        def quant(w, h, fmt):
            grouped, codes, scales = w
            c = slice(h * N_TILE, (h + 1) * N_TILE)
            nc.vector.quantize_mx(
                out=codes[:, c].bitcast(fmt),
                scales=scales[:, c],
                in_=grouped[:, c, :].rearrange("p h j -> p (h j)"),
            )

        def multiply(t, s_fmt, c, w, m_fmt, h, start, stop):
            for d in range(D_TILES):
                s = slice(c * D + d * P, c * D + (d + 1) * P)
                m = slice(h * N_TILE, (h + 1) * N_TILE)
                nc.tensor.matmul_mx(
                    out=acc[d][h][:],
                    lhsT=t[2][:, s].bitcast(s_fmt),
                    lhsT_scale=t[3][:, s],
                    rhs=w[1][:, m].bitcast(m_fmt),
                    rhs_scale=w[2][:, m],
                    start=start,
                    stop=stop,
                )

        def split(w, raw, h, v, j0=0):
            b = h * N_TILE
            if v > 0:
                interleave(nc.vector.tensor_copy, w[0], raw, b, b + v, j0)
            if v < N_TILE:
                interleave(nc.scalar.copy, w[0], raw, b + v, b + N_TILE, j0)

        def wide_pass(w, raw, fmt, t, s_fmt, c, start):
            split(w, raw, 0, 272)
            split(w, raw, 1, 272)
            quant(w, 0, fmt)
            split(w, raw, 2, 272)
            quant(w, 1, fmt)
            quant(w, 2, fmt)
            for h in range(H_TILES):
                multiply(t, s_fmt, c, w, fmt, h, start, False)

        quant_narrow(xt, E4M3)
        wide_pass(wide_tiles("de0"), de0, E5M2, xt, E4M3, 0, True)
        wide_pass(wide_tiles("de1"), de1, E5M2, xt, E4M3, 1, False)
        quant_narrow(drt, E5M2)
        wide_pass(wide_tiles("e0"), e0, E4M3, drt, E5M2, 0, False)

        w = wide_tiles("e1")
        for h in range(H_TILES):
            split(w, e1a, h, 344)

        def finish(d, h):
            m = slice(h * N_TILE, (h + 1) * N_TILE)
            res = keep.tile([P, N_TILE], F32, name="res%d%d" % (d, h))
            nc.vector.tensor_tensor(out=res[:], in0=acc[d][h][:], in1=g[d][:, m], op=mybir.AluOpType.add)
            nc.sync.dma_start(out=out[d * P : (d + 1) * P, m], in_=res[:])

        split(w, e1b, 0, 336, 2)
        quant(w, 0, E4M3)
        multiply(drt, E5M2, 1, w, E4M3, 0, False, True)
        split(w, e1b, 1, 256, 2)
        quant(w, 1, E4M3)
        multiply(drt, E5M2, 1, w, E4M3, 1, False, True)
        split(w, e1b, 2, 0, 2)
        finish(0, 0)
        finish(0, 1)
        quant(w, 2, E4M3)
        multiply(drt, E5M2, 1, w, E4M3, 2, False, True)
        finish(1, 0)
        finish(1, 1)
        finish(0, 2)
        finish(1, 2)
